import numpy as np, ml_dtypes
CORES = [6,15,38,47]
N = 4
import mx_ref
BF = ml_dtypes.bfloat16
def entries(a):
    return np.ascontiguousarray(a.T).reshape(-1)
def table(e):
    return np.ascontiguousarray(np.reshape(e, (-1, 16)).T).astype(np.int32)
def cols(t, e):
    v = np.concatenate([t.reshape(128, -1, 4), np.zeros((128, 1, 4), BF)], axis=1)
    return np.ascontiguousarray(v[:, e]).reshape(128, -1)
def cut(t, i, w=512):
    return t[:, w * i:w * i + w]
def f(rng, *shape):
    return mx_ref.flush((rng.standard_normal(shape, dtype=np.float32) * np.exp2(rng.integers(-2, 3, shape[:-1] + (1,)))).astype(BF))
def wide(rng, *shape, cols=0):
    v = rng.standard_normal(shape, dtype=np.float32) * np.exp2(rng.integers(-12, 13, shape)).astype(np.float32)
    if cols: v *= np.repeat(np.exp2(rng.integers(-cols, cols + 1, shape[:-2] + (1, shape[-1] // 4))) * (rng.random(shape[:-2] + (1, shape[-1] // 4)) > 0.0625), 4, axis=-1).astype(np.float32)
    return mx_ref.flush(v.astype(BF))
C, R, CAPP = 256, 3, 64
def lists(rng, full=False, stay=False, fresh=False, one=False):
    sl = np.full((N, R, N, CAPP), -1); pa = rng.integers(0, C, (N, R, C))
    for t in range(R):
        if stay: continue
        for r in range(N):
            for d in range(N):
                if d == r: continue
                n = CAPP if full else rng.integers(0, CAPP + 1)
                sl[r, t, d, rng.permutation(CAPP)[:n]] = rng.integers(0, C, n)
        for d in range(N):
            far = C + np.flatnonzero(sl[:, t, d].reshape(-1) >= 0)
            pa[d, t, rng.permutation(C)[:far.size]] = far
            if full: continue
            if far.size: pa[d, t, rng.integers(0, C, C // 16)] = rng.choice(far, C // 16)
            pa[d, t, rng.permutation(C)[:C // 2 if fresh else C // 8]] = -1
    if fresh: pa[rng.integers(0, N), rng.integers(0, R)] = -1
    if one:
        o, j = rng.integers(0, N), rng.integers(0, C)
        for t in range(R - 1):
            q, c, k = (o + rng.integers(1, N)) % N, rng.integers(0, CAPP), rng.integers(0, C)
            sl[o, t, q, c] = j; pa[q, t, k] = C + o * CAPP + c
            o, j = q, k
        for q in range(N):
            c = rng.integers(0, CAPP)
            if q != o: sl[o, R - 1, q, c] = j
            pa[q, R - 1] = j if q == o else C + o * CAPP + c
    return {"sl": np.stack([table(sl[r]) for r in range(N)]), "pa": np.stack([table(pa[r]) for r in range(N)])}
def setup_inputs(rng):
    return {"x": f(rng, N, 128, 4 * C * (R + 1)), "w": f(rng, N, 128, 512 * (R + 1)), **lists(rng)}
def setup_inputs_stay(rng):
    return {**setup_inputs(rng), **lists(rng, stay=True)}
def setup_inputs_far(rng):
    return {**setup_inputs(rng), **lists(rng, full=True)}
def setup_inputs_one(rng):
    return {**setup_inputs(rng), **lists(rng, one=True)}
def setup_inputs_fresh(rng):
    return {**setup_inputs(rng), **lists(rng, fresh=True)}
def setup_inputs_spread(rng):
    d = setup_inputs(rng); d["x"] = wide(rng, N, 128, 4 * C * (R + 1), cols=8); return d
def check_inputs(d):
    b = []
    s = [entries(d["sl"][r]).reshape(R, N, CAPP) for r in range(N)]
    for r in range(N):
        p = entries(d["pa"][r]).reshape(R, C)
        if s[r].min() < -1 or s[r].max() >= C or (s[r][:, r] != -1).any(): b.append("sl")
        if p.min() < -1 or p.max() >= C + N * CAPP: b.append("pa"); continue
        for t in range(R):
            slots = np.concatenate([s[q][t, r] for q in range(N)])
            if (slots[p[t][p[t] >= C] - C] < 0).any(): b.append("pa"); break
    return b
def reference(x, w, sl, pa):
    s = [entries(sl[r]).reshape(R, N, CAPP) for r in range(N)]
    p = [entries(pa[r]).reshape(R, C) for r in range(N)]
    cache = [np.ascontiguousarray(cut(x[r], 0, 4 * C)) for r in range(N)]
    y = np.zeros((N, 128, C * (R + 1)), np.float32)
    for t in range(R + 1):
        if t > 0:
            after = []
            for r in range(N):
                slots = [cols(cache[q], s[q][t - 1, r]) for q in range(N)]
                every = np.concatenate([cache[r]] + slots + [cut(x[r], t, 4 * C)], axis=1)
                v = p[r][t - 1]
                after.append(cols(every, np.where(v < 0, C + N * CAPP + np.arange(C), v)))
            cache = after
        for r in range(N):
            y[r][:, C * t:C * t + C] = mx_ref.matmul(mx_ref.quantize(np.ascontiguousarray(cut(w[r], t))), mx_ref.quantize(cache[r]))
    return {"y": y}

@@ -1,0 +1,286 @@
+from concourse.bass import DstId, RemoteDMATransfer
+from concourse.mybir import dt, AluOpType, ActivationFunctionType
+
+C = 256
+CAP = 64
+LAND = 3 * CAP
+NEW = C + LAND
+WIN = NEW + C
+F8, U8 = "float8_e4m3fn_x4", "uint8"
+
+SCRATCH = {
+    "xb": ("sbuf", [128, 4096], "bfloat16"),
+    "wb": ("sbuf", [128, 2048], "bfloat16"),
+    "a0q": ("sbuf", [128, C], F8), "a0s": ("sbuf", [128, C], U8),
+    "wq": ("sbuf", [128, 512], F8), "ws": ("sbuf", [128, 512], U8),
+    "sli": ("sbuf", [128, 48], "int32"), "pai": ("sbuf", [128, 48], "int32"),
+    "ipart": ("sbuf", [128, 48], "int32"), "icol": ("sbuf", [128, 48], "int32"),
+    "idiag": ("sbuf", [128, LAND], "int32"), "imod": ("sbuf", [128, LAND], "int32"),
+    "irep": ("sbuf", [128, 16], "int32"), "ihalf": ("sbuf", [128, 16], "int32"),
+    "irow": ("sbuf", [128, 48], "int32"), "idm": ("sbuf", [128, LAND], "int32"),
+    "ireps": ("sbuf", [128, 16], "int32"), "jnew": ("sbuf", [128, 48], "int32"),
+    "offrep": ("sbuf", [128, 16], "uint16"),
+    "mask": ("sbuf", [128, LAND], "float32"), "keep": ("sbuf", [128, LAND], "float32"),
+    "neg": ("sbuf", [128, 48], "int32"), "negj": ("sbuf", [128, 48], "int32"),
+    "high": ("sbuf", [128, 48], "int32"), "low": ("sbuf", [128, 48], "int32"),
+    "mf": ("sbuf", [128, 48], "float32"), "offm": ("sbuf", [128, 48], "uint16"),
+    "offs": ("sbuf", [128, 36], "uint16"),
+    "yo": ("sbuf", [128, 1024], "float32"), "yw": ("sbuf", [128, WIN], "float32"),
+    "ps": ("psum", [128, 512 * 6], "float32"),
+}
+for _t in (1, 2, 3):
+    SCRATCH["w%dq" % _t] = ("sbuf", [128, WIN], F8)
+    SCRATCH["w%ds" % _t] = ("sbuf", [128, WIN], U8)
+    SCRATCH["s%dq" % _t] = ("sbuf", [128, LAND], F8)
+    SCRATCH["s%ds" % _t] = ("sbuf", [128, LAND], U8)
+    if _t > 1:
+        SCRATCH["rg%d" % _t] = ("sbuf", [128, C], "float32")
+        SCRATCH["tr%d" % _t] = ("sbuf", [128, C], "float32")
+        SCRATCH["gm%d" % _t] = ("sbuf", [128, LAND], "float32")
+        SCRATCH["sc%d" % _t] = ("sbuf", [128, LAND], "float32")
+        SCRATCH["off%d" % _t] = ("sbuf", [128, 12], "uint16")
+
+SEMAPHORES = ["x0", "x1", "x2", "x3", "sl_in", "pa_in", "w01", "w23", "iot", "vc",
+              "os0", "om", "l2", "l3", "qa", "qx0", "qx1", "qx2", "qx3", "qw01", "qw23",
+              "pc1", "pc2", "pc3", "pp1", "pp2", "pp3", "lc1", "lc2", "lc3", "lp1", "lp2", "lp3",
+              "left1", "left2", "left3", "kc1", "kc2", "kp1", "kp2",
+              "m0", "m1", "m2", "m3", "m3l", "e0", "e1", "e2", "e3", "e3l", "fin", "stored"]
+
+
+def send_masks(core, ranks, topo):
+    def way(c):
+        a, b = topo.chip(core), topo.chip(c)
+        return 1 if topo.mates(a, b) else 2 if topo.same_plane(a, b) else 0
+    far = sorted([(way(c), s, c) for s, c in enumerate(ranks) if c != core])
+    eng = [e for e in topo.engines(core, far[0][2]) if all(e in topo.engines(core, c) for _, _, c in far)]
+    q = len(eng) // 4
+    bits = lambda es: sum(1 << e for e in es)
+    codes = [eng[0:2 * q], eng[2 * q:3 * q], eng[3 * q:4 * q]]
+    plane = [eng[0:q], eng[q:2 * q], eng[2 * q:4 * q]]
+    return [(s, codes[i], plane[i], bits(codes[i]), bits(plane[i])) for i, (_, s, _) in enumerate(far)]
+
+
+def rank_program(g, core, T, topo):
+    r = T.rank_of(core)
+    if r is None:
+        return
+    v, sc, te, sy, sem = g.vector, g.scalar, g.tensor, g.sync, T.sem
+    Copy = ActivationFunctionType.Copy
+    ranks = list(T.cores)
+    place = lambda owner, other: other if other < owner else other - 1
+
+    sy.dma_start(T.xb[:, 0:1024], T.x[:, 0:1024]).then_inc(sem.x0, 16)
+    for k in range(8):
+        q = sc if k < 6 else sy
+        q.dma_start(T.sli[16 * k:16 * k + 16, :], T.sl[:]).then_inc(sem.sl_in, 16)
+    for k in range(8):
+        sy.dma_start(T.pai[16 * k:16 * k + 16, :], T.pa[:]).then_inc(sem.pa_in, 16)
+    sy.dma_start(T.xb[:, 1024:2048], T.x[:, 1024:2048]).then_inc(sem.x1, 16)
+
+    g.iota(T.ipart[:], [[0, 48]], 0, 1).then_inc(sem.iot, 1)
+    g.iota(T.icol[:], [[0, 3], [16, 16]], NEW, 0).then_inc(sem.iot, 1)
+    g.iota(T.irep[:], [[2, 8], [0, 2]], 0, 0).then_inc(sem.iot, 1)
+    g.iota(T.imod[:], [[0, 12], [1, 16]], 0, 0).then_inc(sem.iot, 1)
+    g.iota(T.idiag[:], [[1, LAND]], 0, -1).then_inc(sem.iot, 1)
+
+    nv = [0]
+
+    def chain(ins):
+        ins.then_inc(sem.vc, 1)
+        nv[0] += 1
+
+    def settle():
+        v.wait_ge(sem.vc, nv[0])
+
+    v.wait_ge(sem.iot, 5)
+    chain(v.tensor_scalar(T.irow[:], T.ipart[:], 15, None, AluOpType.bitwise_and))
+    chain(v.tensor_scalar(T.ihalf[:], T.ipart[:, 0:16], 4, 1, AluOpType.arith_shift_right, AluOpType.bitwise_and))
+    chain(v.tensor_scalar(T.idm[:], T.idiag[:], 15, None, AluOpType.bitwise_and))
+    chain(v.tensor_scalar(T.keep[:], T.imod[:], 0, None, AluOpType.not_equal))
+    settle()
+    chain(v.tensor_tensor(T.jnew[:], T.irow[:], T.icol[:], AluOpType.add))
+    chain(v.tensor_tensor(T.ireps[:], T.irep[:], T.ihalf[:], AluOpType.add))
+    chain(v.tensor_scalar(T.mask[:], T.idm[:], 0, None, AluOpType.is_equal))
+    settle()
+    chain(v.tensor_copy(T.offrep[:], T.ireps[:]))
+
+    def slots(t):
+        out = []
+        a, o = 16 * (t - 1), 12 * (t - 1)
+        if r > 0:
+            out.append(v.tensor_copy(T.offs[:, o:o + 4 * r], T.sli[:, a:a + 4 * r]))
+        if r < 3:
+            out.append(v.tensor_copy(T.offs[:, o + 4 * r:o + 12], T.sli[:, a + 4 * r + 4:a + 16]))
+        return out
+
+    v.wait_ge(sem.sl_in, 128)
+    n0 = 0
+    for i in slots(1):
+        i.then_inc(sem.os0, 1)
+        n0 += 1
+    v.wait_ge(sem.x0, 16)
+    v.quantize_mx(T.a0q[:], T.a0s[:], T.xb[:, 0:1024]).then_inc(sem.qa, 1)
+    v.wait_ge(sem.os0, n0)
+    v.wait_ge(sem.qa, 1)
+    v.tensor_copy(T.s1q[:].bitcast(dt.uint32), T.a0q[:].bitcast(dt.uint32).indirect(T.offs[:, 0:12])).then_inc(sem.pc1, 1)
+    sc.wait_ge(sem.os0, n0)
+    sc.wait_ge(sem.qa, 1)
+    sc.activation(T.s1s[:], T.a0s[:].indirect(T.offs[:, 0:12]), Copy).then_inc(sem.pp1, 1)
+
+    plan = send_masks(core, ranks, topo)
+    got_c, got_p = 0, 0
+    for s, c in enumerate(ranks):
+        if c != core:
+            for d, ec, ep, _, _ in send_masks(c, ranks, topo):
+                if d == r:
+                    got_c += len(ec)
+                    got_p += len(ep)
+    left = sum(len(p[1]) + len(p[2]) for p in plan)
+
+    def send(t, n_planes):
+        for part in (0, 1):
+            g.wait_ge(sem["pp%d" % t] if part else sem["pc%d" % t], n_planes if part else 1)
+            moves = []
+            for d, _, _, mc, mp in plan:
+                rid, pid, _ = topo.addr(ranks[d])
+                a, b = CAP * place(r, d), C + CAP * place(d, r)
+                if part:
+                    src, dst = T["s%ds" % t][:, a:a + CAP], T["w%ds" % t][:, b:b + CAP]
+                else:
+                    src = T["s%dq" % t][:, a:a + CAP].bitcast(dt.uint8)
+                    dst = T["w%dq" % t][:, b:b + CAP].bitcast(dt.uint8)
+                moves.append(RemoteDMATransfer(dst_ids=[DstId(rid=rid, pnc=pid)], dma_engine_mask=mp if part else mc,
+                                               remote_sem=sem["lp%d" % t] if part else sem["lc%d" % t],
+                                               src=src, dst=dst))
+            g.remote_dma_fused(moves, local_sem=sem["left%d" % t])
+
+    send(1, 1)
+
+    v.wait_ge(sem.pa_in, 128)
+    chain(v.tensor_scalar(T.neg[:], T.pai[:], 0, None, AluOpType.is_lt))
+    if r < 3:
+        chain(v.tensor_scalar(T.high[:], T.pai[:], C + CAP * (r + 1), -CAP, AluOpType.is_ge, AluOpType.mult))
+    settle()
+    chain(v.tensor_tensor(T.negj[:], T.neg[:], T.jnew[:], AluOpType.mult))
+    low = T.pai
+    if r < 3:
+        chain(v.tensor_tensor(T.low[:], T.pai[:], T.high[:], AluOpType.add))
+        low = T.low
+    for t in (2, 3):
+        for i in slots(t):
+            chain(i)
+    settle()
+    chain(v.tensor_tensor(T.mf[:], low[:], T.negj[:], AluOpType.max))
+    settle()
+
+    def compose(t):
+        rg, tr, gm, ss, off = T["rg%d" % t], T["tr%d" % t], T["gm%d" % t], T["sc%d" % t], T["off%d" % t]
+        a, o = 16 * (t - 2), 12 * (t - 1)
+        chain(v.tensor_copy(rg[:], T.mf[:, a:a + 16].indirect(T.offrep[:, 0:16])))
+        settle()
+        chain(v.transpose(tr[:], rg[:]))
+        settle()
+        chain(v.tensor_tensor(gm[:], tr[:].indirect(T.offs[:, o:o + 12]), T.mask[:], AluOpType.mult))
+        settle()
+        chain(v.tensor_tensor_scan(ss[:], T.keep[:], gm[:], 0.0, AluOpType.mult, AluOpType.add))
+        settle()
+        v.tensor_copy(off[:], ss[:, 15:LAND:16]).then_inc(sem["l%d" % t], 1)
+
+    compose(2)
+    v.tensor_copy(T.offm[:], T.mf[:]).then_inc(sem.om, 1)
+    v.quantize_mx(T.w1q[:, 0:C], T.w1s[:, 0:C], T.xb[:, 0:1024]).then_inc(sem.qx0, 1)
+    v.wait_ge(sem.x1, 16)
+    v.quantize_mx(T.w1q[:, NEW:WIN], T.w1s[:, NEW:WIN], T.xb[:, 1024:2048]).then_inc(sem.qx1, 1)
+
+    sy.wait_ge(sem.left1, left)
+    sy.dma_start(T.xb[:, 2048:3072], T.x[:, 2048:3072]).then_inc(sem.x2, 16)
+    sy.dma_start(T.wb[:, 0:1024], T.w[:, 0:1024]).then_inc(sem.w01, 16)
+    sy.wait_ge(sem.left2, left)
+    sy.dma_start(T.xb[:, 3072:4096], T.x[:, 3072:4096]).then_inc(sem.x3, 16)
+    sy.dma_start(T.wb[:, 1024:2048], T.w[:, 1024:2048]).then_inc(sem.w23, 16)
+
+    def product(t, src, ssrc, a, n, bank, done):
+        te.matmul_mx(T.ps[:, 512 * bank:512 * bank + n], T.wq[:, 128 * t:128 * t + 128], T.ws[:, 128 * t:128 * t + 128],
+                     src[:, a:a + n], ssrc[:, a:a + n], True, True).then_inc(done, 1)
+
+    for t in (2, 3):
+        wq, ws = T["w%dq" % (t - 1)], T["w%ds" % (t - 1)]
+        sq, ss = T["s%dq" % t], T["s%ds" % t]
+        off, u = T["off%d" % t], t - 1
+        qown, qnew = (sem.qx0, sem.qx1) if t == 2 else (sem.kc1, sem.qx2)
+        pown = sem.qx0 if t == 2 else sem.kp1
+        v.wait_ge(qown, 1)
+        v.wait_ge(qnew, 1)
+        v.wait_ge(sem["l%d" % t], 1)
+        v.wait_ge(sem["lc%d" % u], got_c)
+        v.tensor_copy(sq[:, 0:96].bitcast(dt.uint32), wq[:].bitcast(dt.uint32).indirect(off[:, 0:6])).then_inc(sem.vc, 1)
+        v.tensor_copy(sq[:, 96:192].bitcast(dt.uint32), wq[:].bitcast(dt.uint32).indirect(off[:, 6:12])).then_inc(sem["pc%d" % t], 1)
+        nv[0] += 1
+        g.wait_ge(sem.vc, nv[0])
+        sc.wait_ge(pown, 1)
+        sc.wait_ge(qnew, 1)
+        sc.wait_ge(sem["l%d" % t], 1)
+        sc.wait_ge(sem["lp%d" % u], got_p)
+        sc.activation(ss[:, 0:96], ws[:].indirect(off[:, 0:6]), Copy).then_inc(sem["pp%d" % t], 1)
+        v.wait_ge(pown, 1)
+        v.wait_ge(sem["lp%d" % u], got_p)
+        v.tensor_copy(ss[:, 96:192], ws[:].indirect(off[:, 6:12])).then_inc(sem["pp%d" % t], 1)
+        send(t, 2)
+        kq, ks = T["w%dq" % t], T["w%ds" % t]
+        om = T.offm[:, 16 * (t - 2):16 * (t - 1)]
+        v.wait_ge(sem.om, 1)
+        v.tensor_copy(kq[:, 0:C].bitcast(dt.uint32), wq[:].bitcast(dt.uint32).indirect(om)).then_inc(sem["kc%d" % u], 1)
+        sc.wait_ge(sem.om, 1)
+        sc.activation(ks[:, 0:C], ws[:].indirect(om), Copy).then_inc(sem["kp%d" % u], 1)
+        if t == 2:
+            compose(3)
+            v.wait_ge(sem.x2, 16)
+            v.quantize_mx(T.w2q[:, NEW:WIN], T.w2s[:, NEW:WIN], T.xb[:, 2048:3072]).then_inc(sem.qx2, 1)
+            v.wait_ge(sem.w01, 16)
+            v.quantize_mx(T.wq[:, 0:256], T.ws[:, 0:256], T.wb[:, 0:1024]).then_inc(sem.qw01, 1)
+            te.wait_ge(sem.qa, 1)
+            te.wait_ge(sem.qw01, 1)
+            product(0, T.a0q, T.a0s, 0, C, 0, sem.m0)
+            te.wait_ge(sem.kc1, 1)
+            te.wait_ge(sem.kp1, 1)
+            product(1, T.w2q, T.w2s, 0, C, 1, sem.m1)
+            for b in (0, 1):
+                sc.wait_ge(sem["m%d" % b], 1)
+                sc.activation(T.yo[:, C * b:C * b + C], T.ps[:, 512 * b:512 * b + C], Copy).then_inc(sem["e%d" % b], 1)
+        else:
+            v.wait_ge(sem.x3, 16)
+            v.quantize_mx(T.w3q[:, NEW:WIN], T.w3s[:, NEW:WIN], T.xb[:, 3072:4096]).then_inc(sem.qx3, 1)
+            v.wait_ge(sem.w23, 16)
+            v.quantize_mx(T.wq[:, 256:512], T.ws[:, 256:512], T.wb[:, 1024:2048]).then_inc(sem.qw23, 1)
+            te.wait_ge(sem.kc2, 1)
+            te.wait_ge(sem.kp2, 1)
+            te.wait_ge(sem.qw23, 1)
+            te.wait_ge(sem.qx3, 1)
+            product(3, T.w3q, T.w3s, 0, C, 3, sem.m3)
+            product(3, T.w3q, T.w3s, NEW, C, 4, sem.m3)
+            product(2, T.w3q, T.w3s, 0, C, 2, sem.m2)
+            sc.wait_ge(sem.m3, 2)
+            sc.activation(T.yw[:, 0:C], T.ps[:, 512 * 3:512 * 3 + C], Copy).then_inc(sem.e3, 1)
+            sc.activation(T.yw[:, NEW:WIN], T.ps[:, 512 * 4:512 * 4 + C], Copy).then_inc(sem.e3, 1)
+            sc.wait_ge(sem.m2, 1)
+            sc.activation(T.yo[:, 2 * C:3 * C], T.ps[:, 1024:1024 + C], Copy).then_inc(sem.e2, 1)
+
+    sy.wait_ge(sem.left3, left)
+    for b in (0, 1, 2):
+        sy.wait_ge(sem["e%d" % b], 1)
+        sy.dma_start(T.y[:, C * b:C * b + C], T.yo[:, C * b:C * b + C]).then_inc(sem.stored, 16)
+
+    te.wait_ge(sem.lc3, got_c)
+    te.wait_ge(sem.lp3, got_p)
+    product(3, T.w3q, T.w3s, C, LAND, 5, sem.m3l)
+    v.wait_ge(sem.m3l, 1)
+    v.tensor_copy(T.yw[:, C:NEW], T.ps[:, 512 * 5:512 * 5 + LAND]).then_inc(sem.e3l, 1)
+    v.wait_ge(sem.e3, 2)
+    v.wait_ge(sem.e3l, 1)
+    v.tensor_copy(T.yo[:, 3 * C + 128:4 * C], T.yw[:].indirect(T.offm[:, 40:48])).then_inc(sem.fin, 1)
+    sc.wait_ge(sem.e3, 2)
+    sc.wait_ge(sem.e3l, 1)
+    sc.activation(T.yo[:, 3 * C:3 * C + 128], T.yw[:].indirect(T.offm[:, 32:40]), Copy).then_inc(sem.fin, 1)
+    sy.wait_ge(sem.fin, 2)
+    sy.dma_start(T.y[:, 3 * C:4 * C], T.yo[:, 3 * C:4 * C]).then_inc(sem.stored, 16)
+    sy.wait_ge(sem.stored, 64)

@@ -14,17 +14,15 @@ SCRATCH = {
     "a0q": ("sbuf", [128, C], F8), "a0s": ("sbuf", [128, C], U8),
     "wq": ("sbuf", [128, 512], F8), "ws": ("sbuf", [128, 512], U8),
     "sli": ("sbuf", [128, 48], "int32"), "pai": ("sbuf", [128, 48], "int32"),
-    "ipart": ("sbuf", [128, 48], "int32"), "icol": ("sbuf", [128, 48], "int32"),
-    "idiag": ("sbuf", [128, LAND], "int32"), "imod": ("sbuf", [128, LAND], "int32"),
-    "irep": ("sbuf", [128, 16], "int32"), "ihalf": ("sbuf", [128, 16], "int32"),
-    "irow": ("sbuf", [128, 48], "int32"), "idm": ("sbuf", [128, LAND], "int32"),
-    "ireps": ("sbuf", [128, 16], "int32"), "jnew": ("sbuf", [128, 48], "int32"),
-    "offrep": ("sbuf", [128, 16], "uint16"),
+    "ipart": ("sbuf", [128, 1], "int32"), "icol": ("sbuf", [128, 48], "int32"),
+    "imod": ("sbuf", [128, LAND], "float32"), "irep": ("sbuf", [128, 16], "int32"),
+    "ibit": ("sbuf", [128, 2], "int32"), "fbit": ("sbuf", [128, 2], "float32"),
+    "jnew": ("sbuf", [128, 48], "int32"), "offrep": ("sbuf", [128, 16], "uint16"),
     "mask": ("sbuf", [128, LAND], "float32"), "keep": ("sbuf", [128, LAND], "float32"),
     "neg": ("sbuf", [128, 48], "int32"), "negj": ("sbuf", [128, 48], "int32"),
     "high": ("sbuf", [128, 48], "int32"), "low": ("sbuf", [128, 48], "int32"),
     "mf": ("sbuf", [128, 48], "float32"), "offm": ("sbuf", [128, 48], "uint16"),
-    "offs": ("sbuf", [128, 36], "uint16"),
+    "offs": ("sbuf", [128, 48], "uint16"),
     "yo": ("sbuf", [128, 1024], "float32"), "yw": ("sbuf", [128, WIN], "float32"),
     "ps": ("psum", [128, 512 * 6], "float32"),
 }
@@ -41,7 +39,7 @@ for _t in (1, 2, 3):
         SCRATCH["off%d" % _t] = ("sbuf", [128, 12], "uint16")
 
 SEMAPHORES = ["x0", "x1", "x2", "x3", "sl_in", "pa_in", "w01", "w23", "iot", "vc",
-              "os0", "om", "l2", "l3", "qa", "qx0", "qx1", "qx2", "qx3", "qw01", "qw23",
+              "ofs", "om", "mf", "rg2", "rg3", "l2", "l3", "qa", "qx0", "qx1", "qx2", "qx3", "qw01", "qw23",
               "pc1", "pc2", "pc3", "pp1", "pp2", "pp3", "lc1", "lc2", "lc3", "lp1", "lp2", "lp3",
               "left1", "left2", "left3", "kc1", "kc2", "kp1", "kp2",
               "m0", "m1", "m2", "m3", "m3l", "e0", "e1", "e2", "e3", "e3l", "fin", "stored"]
@@ -53,11 +51,11 @@ def send_masks(core, ranks, topo):
         return 1 if topo.mates(a, b) else 2 if topo.same_plane(a, b) else 0
     far = sorted([(way(c), s, c) for s, c in enumerate(ranks) if c != core])
     eng = [e for e in topo.engines(core, far[0][2]) if all(e in topo.engines(core, c) for _, _, c in far)]
-    q = len(eng) // 4
-    bits = lambda es: sum(1 << e for e in es)
-    codes = [eng[0:2 * q], eng[2 * q:3 * q], eng[3 * q:4 * q]]
-    plane = [eng[0:q], eng[q:2 * q], eng[2 * q:4 * q]]
-    return [(s, codes[i], plane[i], bits(codes[i]), bits(plane[i])) for i, (_, s, _) in enumerate(far)]
+    one, two = eng[0::2], eng[1::2]
+    h = len(one) // 2
+    codes = [one, two[:h], two[h:]]
+    plane = [one[:h], one[h:], two]
+    return [(s, codes[i], plane[i]) for i, (_, s, _) in enumerate(far)]
 
 
 def rank_program(g, core, T, topo):
@@ -76,12 +74,14 @@ def rank_program(g, core, T, topo):
     for k in range(8):
         sy.dma_start(T.pai[16 * k:16 * k + 16, :], T.pa[:]).then_inc(sem.pa_in, 16)
     sy.dma_start(T.xb[:, 1024:2048], T.x[:, 1024:2048]).then_inc(sem.x1, 16)
+    sy.dma_start(T.xb[:, 2048:3072], T.x[:, 2048:3072]).then_inc(sem.x2, 16)
+    sy.dma_start(T.xb[:, 3072:4096], T.x[:, 3072:4096]).then_inc(sem.x3, 16)
+    sy.dma_start(T.wb[:, 1024:2048], T.w[:, 1024:2048]).then_inc(sem.w23, 16)
 
-    g.iota(T.ipart[:], [[0, 48]], 0, 1).then_inc(sem.iot, 1)
-    g.iota(T.icol[:], [[0, 3], [16, 16]], NEW, 0).then_inc(sem.iot, 1)
+    g.iota(T.ipart[:], [[0, 1]], 0, 1).then_inc(sem.iot, 1)
     g.iota(T.irep[:], [[2, 8], [0, 2]], 0, 0).then_inc(sem.iot, 1)
-    g.iota(T.imod[:], [[0, 12], [1, 16]], 0, 0).then_inc(sem.iot, 1)
-    g.iota(T.idiag[:], [[1, LAND]], 0, -1).then_inc(sem.iot, 1)
+    g.iota(T.icol[:], [[0, 3], [16, 16]], NEW, 0).then_inc(sem.iot, 1)
+    g.iota(T.imod[:], [[0, 12], [1, 16]], 0, 0, allow_small_or_imprecise_dtypes=True).then_inc(sem.iot, 1)
 
     nv = [0]
 
@@ -92,56 +92,49 @@ def rank_program(g, core, T, topo):
     def settle():
         v.wait_ge(sem.vc, nv[0])
 
-    v.wait_ge(sem.iot, 5)
-    chain(v.tensor_scalar(T.irow[:], T.ipart[:], 15, None, AluOpType.bitwise_and))
-    chain(v.tensor_scalar(T.ihalf[:], T.ipart[:, 0:16], 4, 1, AluOpType.arith_shift_right, AluOpType.bitwise_and))
-    chain(v.tensor_scalar(T.idm[:], T.idiag[:], 15, None, AluOpType.bitwise_and))
-    chain(v.tensor_scalar(T.keep[:], T.imod[:], 0, None, AluOpType.not_equal))
+    v.wait_ge(sem.iot, 4)
+    chain(v.tensor_scalar(T.ibit[:, 0:1], T.ipart[:], 15, None, AluOpType.bitwise_and))
+    chain(v.tensor_scalar(T.ibit[:, 1:2], T.ipart[:], 4, 1, AluOpType.arith_shift_right, AluOpType.bitwise_and))
     settle()
-    chain(v.tensor_tensor(T.jnew[:], T.irow[:], T.icol[:], AluOpType.add))
-    chain(v.tensor_tensor(T.ireps[:], T.irep[:], T.ihalf[:], AluOpType.add))
-    chain(v.tensor_scalar(T.mask[:], T.idm[:], 0, None, AluOpType.is_equal))
+    chain(v.tensor_copy(T.fbit[:], T.ibit[:]))
+    chain(v.tensor_scalar(T.keep[:], T.imod[:], 0.0, None, AluOpType.not_equal))
     settle()
-    chain(v.tensor_copy(T.offrep[:], T.ireps[:]))
+    chain(v.tensor_scalar(T.jnew[:], T.icol[:], T.fbit[:, 0:1], None, AluOpType.add))
+    chain(v.tensor_scalar(T.offrep[:], T.irep[:], T.fbit[:, 1:2], None, AluOpType.add))
+    chain(v.tensor_scalar(T.mask[:], T.imod[:], T.fbit[:, 0:1], None, AluOpType.is_equal))
 
-    def slots(t):
-        out = []
-        a, o = 16 * (t - 1), 12 * (t - 1)
-        if r > 0:
-            out.append(v.tensor_copy(T.offs[:, o:o + 4 * r], T.sli[:, a:a + 4 * r]))
-        if r < 3:
-            out.append(v.tensor_copy(T.offs[:, o + 4 * r:o + 12], T.sli[:, a + 4 * r + 4:a + 16]))
-        return out
+    runs = [(a, b, o) for a, b, o in ((0, 4 * r, 0), (4 * r + 4, 16, 4 * r)) if b > a]
 
     v.wait_ge(sem.sl_in, 128)
-    n0 = 0
-    for i in slots(1):
-        i.then_inc(sem.os0, 1)
-        n0 += 1
+    v.tensor_copy(T.offs[:], T.sli[:]).then_inc(sem.ofs, 1)
     v.wait_ge(sem.x0, 16)
     v.quantize_mx(T.a0q[:], T.a0s[:], T.xb[:, 0:1024]).then_inc(sem.qa, 1)
-    v.wait_ge(sem.os0, n0)
+    v.wait_ge(sem.ofs, 1)
     v.wait_ge(sem.qa, 1)
-    v.tensor_copy(T.s1q[:].bitcast(dt.uint32), T.a0q[:].bitcast(dt.uint32).indirect(T.offs[:, 0:12])).then_inc(sem.pc1, 1)
-    sc.wait_ge(sem.os0, n0)
+    sc.wait_ge(sem.ofs, 1)
     sc.wait_ge(sem.qa, 1)
-    sc.activation(T.s1s[:], T.a0s[:].indirect(T.offs[:, 0:12]), Copy).then_inc(sem.pp1, 1)
+    for a, b, o in runs:
+        m, n = 16 * o, 16 * (o + b - a)
+        v.tensor_copy(T.s1q[:, m:n].bitcast(dt.uint32),
+                      T.a0q[:].bitcast(dt.uint32).indirect(T.offs[:, a:b])).then_inc(sem.pc1, 1)
+        sc.activation(T.s1s[:, m:n], T.a0s[:].indirect(T.offs[:, a:b]), Copy).then_inc(sem.pp1, 1)
 
     plan = send_masks(core, ranks, topo)
+    bits = lambda es: sum(1 << e for e in es)
     got_c, got_p = 0, 0
     for s, c in enumerate(ranks):
         if c != core:
-            for d, ec, ep, _, _ in send_masks(c, ranks, topo):
+            for d, ec, ep in send_masks(c, ranks, topo):
                 if d == r:
                     got_c += len(ec)
                     got_p += len(ep)
     left = sum(len(p[1]) + len(p[2]) for p in plan)
 
-    def send(t, n_planes):
+    def send(t, n_picks):
         for part in (0, 1):
-            g.wait_ge(sem["pp%d" % t] if part else sem["pc%d" % t], n_planes if part else 1)
+            g.wait_ge(sem["pp%d" % t] if part else sem["pc%d" % t], n_picks)
             moves = []
-            for d, _, _, mc, mp in plan:
+            for d, ec, ep in plan:
                 rid, pid, _ = topo.addr(ranks[d])
                 a, b = CAP * place(r, d), C + CAP * place(d, r)
                 if part:
@@ -149,12 +142,12 @@ def rank_program(g, core, T, topo):
                 else:
                     src = T["s%dq" % t][:, a:a + CAP].bitcast(dt.uint8)
                     dst = T["w%dq" % t][:, b:b + CAP].bitcast(dt.uint8)
-                moves.append(RemoteDMATransfer(dst_ids=[DstId(rid=rid, pnc=pid)], dma_engine_mask=mp if part else mc,
+                moves.append(RemoteDMATransfer(dst_ids=[DstId(rid=rid, pnc=pid)], dma_engine_mask=bits(ep if part else ec),
                                                remote_sem=sem["lp%d" % t] if part else sem["lc%d" % t],
                                                src=src, dst=dst))
             g.remote_dma_fused(moves, local_sem=sem["left%d" % t])
 
-    send(1, 1)
+    send(1, len(runs))
 
     v.wait_ge(sem.pa_in, 128)
     chain(v.tensor_scalar(T.neg[:], T.pai[:], 0, None, AluOpType.is_lt))
@@ -166,38 +159,36 @@ def rank_program(g, core, T, topo):
     if r < 3:
         chain(v.tensor_tensor(T.low[:], T.pai[:], T.high[:], AluOpType.add))
         low = T.low
+    settle()
+    v.tensor_tensor(T.mf[:], low[:], T.negj[:], AluOpType.max).then_inc(sem.mf, 1)
+    sc.wait_ge(sem.mf, 1)
     for t in (2, 3):
-        for i in slots(t):
-            chain(i)
-    settle()
-    chain(v.tensor_tensor(T.mf[:], low[:], T.negj[:], AluOpType.max))
-    settle()
+        a = 16 * (t - 2)
+        sc.activation(T["rg%d" % t][:], T.mf[:, a:a + 16].indirect(T.offrep[:, 0:16]), Copy).then_inc(sem["rg%d" % t], 1)
 
     def compose(t):
-        rg, tr, gm, ss, off = T["rg%d" % t], T["tr%d" % t], T["gm%d" % t], T["sc%d" % t], T["off%d" % t]
-        a, o = 16 * (t - 2), 12 * (t - 1)
-        chain(v.tensor_copy(rg[:], T.mf[:, a:a + 16].indirect(T.offrep[:, 0:16])))
+        tr, gm, ss, off = T["tr%d" % t], T["gm%d" % t], T["sc%d" % t], T["off%d" % t]
+        v.wait_ge(sem["rg%d" % t], 1)
+        chain(v.transpose(tr[:], T["rg%d" % t][:]))
         settle()
-        chain(v.transpose(tr[:], rg[:]))
-        settle()
-        chain(v.tensor_tensor(gm[:], tr[:].indirect(T.offs[:, o:o + 12]), T.mask[:], AluOpType.mult))
+        for a, b, o in runs:
+            m, n, c = 16 * o, 16 * (o + b - a), 16 * (t - 1)
+            chain(v.tensor_tensor(gm[:, m:n], tr[:].indirect(T.offs[:, c + a:c + b]), T.mask[:, m:n], AluOpType.mult))
         settle()
         chain(v.tensor_tensor_scan(ss[:], T.keep[:], gm[:], 0.0, AluOpType.mult, AluOpType.add))
         settle()
         v.tensor_copy(off[:], ss[:, 15:LAND:16]).then_inc(sem["l%d" % t], 1)
 
-    compose(2)
-    v.tensor_copy(T.offm[:], T.mf[:]).then_inc(sem.om, 1)
     v.quantize_mx(T.w1q[:, 0:C], T.w1s[:, 0:C], T.xb[:, 0:1024]).then_inc(sem.qx0, 1)
+    v.wait_ge(sem.mf, 1)
+    v.tensor_copy(T.offm[:], T.mf[:]).then_inc(sem.om, 1)
+    compose(2)
     v.wait_ge(sem.x1, 16)
     v.quantize_mx(T.w1q[:, NEW:WIN], T.w1s[:, NEW:WIN], T.xb[:, 1024:2048]).then_inc(sem.qx1, 1)
 
     sy.wait_ge(sem.left1, left)
-    sy.dma_start(T.xb[:, 2048:3072], T.x[:, 2048:3072]).then_inc(sem.x2, 16)
-    sy.dma_start(T.wb[:, 0:1024], T.w[:, 0:1024]).then_inc(sem.w01, 16)
     sy.wait_ge(sem.left2, left)
-    sy.dma_start(T.xb[:, 3072:4096], T.x[:, 3072:4096]).then_inc(sem.x3, 16)
-    sy.dma_start(T.wb[:, 1024:2048], T.w[:, 1024:2048]).then_inc(sem.w23, 16)
+    sy.dma_start(T.wb[:, 0:1024], T.w[:, 0:1024]).then_inc(sem.w01, 16)
 
     def product(t, src, ssrc, a, n, bank, done):
         te.matmul_mx(T.ps[:, 512 * bank:512 * bank + n], T.wq[:, 128 * t:128 * t + 128], T.ws[:, 128 * t:128 * t + 128],
@@ -207,25 +198,15 @@ def rank_program(g, core, T, topo):
         wq, ws = T["w%dq" % (t - 1)], T["w%ds" % (t - 1)]
         sq, ss = T["s%dq" % t], T["s%ds" % t]
         off, u = T["off%d" % t], t - 1
-        qown, qnew = (sem.qx0, sem.qx1) if t == 2 else (sem.kc1, sem.qx2)
-        pown = sem.qx0 if t == 2 else sem.kp1
-        v.wait_ge(qown, 1)
-        v.wait_ge(qnew, 1)
-        v.wait_ge(sem["l%d" % t], 1)
-        v.wait_ge(sem["lc%d" % u], got_c)
-        v.tensor_copy(sq[:, 0:96].bitcast(dt.uint32), wq[:].bitcast(dt.uint32).indirect(off[:, 0:6])).then_inc(sem.vc, 1)
-        v.tensor_copy(sq[:, 96:192].bitcast(dt.uint32), wq[:].bitcast(dt.uint32).indirect(off[:, 6:12])).then_inc(sem["pc%d" % t], 1)
-        nv[0] += 1
-        g.wait_ge(sem.vc, nv[0])
-        sc.wait_ge(pown, 1)
-        sc.wait_ge(qnew, 1)
-        sc.wait_ge(sem["l%d" % t], 1)
-        sc.wait_ge(sem["lp%d" % u], got_p)
-        sc.activation(ss[:, 0:96], ws[:].indirect(off[:, 0:6]), Copy).then_inc(sem["pp%d" % t], 1)
-        v.wait_ge(pown, 1)
-        v.wait_ge(sem["lp%d" % u], got_p)
-        v.tensor_copy(ss[:, 96:192], ws[:].indirect(off[:, 6:12])).then_inc(sem["pp%d" % t], 1)
-        send(t, 2)
+        v.wait_ge(sem.qx0 if t == 2 else sem.kc1, 1)
+        sc.wait_ge(sem.qx0 if t == 2 else sem.kp1, 1)
+        for q, landed, n in ((v, sem["lc%d" % u], got_c), (sc, sem["lp%d" % u], got_p)):
+            q.wait_ge(sem.qx1 if t == 2 else sem.qx2, 1)
+            q.wait_ge(sem["l%d" % t], 1)
+            q.wait_ge(landed, n)
+        v.tensor_copy(sq[:].bitcast(dt.uint32), wq[:].bitcast(dt.uint32).indirect(off[:, 0:12])).then_inc(sem["pc%d" % t], 1)
+        sc.activation(ss[:], ws[:].indirect(off[:, 0:12]), Copy).then_inc(sem["pp%d" % t], 1)
+        send(t, 1)
         kq, ks = T["w%dq" % t], T["w%ds" % t]
         om = T.offm[:, 16 * (t - 2):16 * (t - 1)]
         v.wait_ge(sem.om, 1)
@@ -236,37 +217,36 @@ def rank_program(g, core, T, topo):
             compose(3)
             v.wait_ge(sem.x2, 16)
             v.quantize_mx(T.w2q[:, NEW:WIN], T.w2s[:, NEW:WIN], T.xb[:, 2048:3072]).then_inc(sem.qx2, 1)
-            v.wait_ge(sem.w01, 16)
-            v.quantize_mx(T.wq[:, 0:256], T.ws[:, 0:256], T.wb[:, 0:1024]).then_inc(sem.qw01, 1)
-            te.wait_ge(sem.qa, 1)
-            te.wait_ge(sem.qw01, 1)
-            product(0, T.a0q, T.a0s, 0, C, 0, sem.m0)
-            te.wait_ge(sem.kc1, 1)
-            te.wait_ge(sem.kp1, 1)
-            product(1, T.w2q, T.w2s, 0, C, 1, sem.m1)
-            for b in (0, 1):
-                sc.wait_ge(sem["m%d" % b], 1)
-                sc.activation(T.yo[:, C * b:C * b + C], T.ps[:, 512 * b:512 * b + C], Copy).then_inc(sem["e%d" % b], 1)
-        else:
-            v.wait_ge(sem.x3, 16)
-            v.quantize_mx(T.w3q[:, NEW:WIN], T.w3s[:, NEW:WIN], T.xb[:, 3072:4096]).then_inc(sem.qx3, 1)
-            v.wait_ge(sem.w23, 16)
-            v.quantize_mx(T.wq[:, 256:512], T.ws[:, 256:512], T.wb[:, 1024:2048]).then_inc(sem.qw23, 1)
-            te.wait_ge(sem.kc2, 1)
-            te.wait_ge(sem.kp2, 1)
-            te.wait_ge(sem.qw23, 1)
-            te.wait_ge(sem.qx3, 1)
-            product(3, T.w3q, T.w3s, 0, C, 3, sem.m3)
-            product(3, T.w3q, T.w3s, NEW, C, 4, sem.m3)
-            product(2, T.w3q, T.w3s, 0, C, 2, sem.m2)
-            sc.wait_ge(sem.m3, 2)
-            sc.activation(T.yw[:, 0:C], T.ps[:, 512 * 3:512 * 3 + C], Copy).then_inc(sem.e3, 1)
-            sc.activation(T.yw[:, NEW:WIN], T.ps[:, 512 * 4:512 * 4 + C], Copy).then_inc(sem.e3, 1)
-            sc.wait_ge(sem.m2, 1)
-            sc.activation(T.yo[:, 2 * C:3 * C], T.ps[:, 1024:1024 + C], Copy).then_inc(sem.e2, 1)
 
+    v.wait_ge(sem.w23, 16)
+    v.quantize_mx(T.wq[:, 256:512], T.ws[:, 256:512], T.wb[:, 1024:2048]).then_inc(sem.qw23, 1)
+    v.wait_ge(sem.x3, 16)
+    v.quantize_mx(T.w3q[:, NEW:WIN], T.w3s[:, NEW:WIN], T.xb[:, 3072:4096]).then_inc(sem.qx3, 1)
+    v.wait_ge(sem.w01, 16)
+    v.quantize_mx(T.wq[:, 0:256], T.ws[:, 0:256], T.wb[:, 0:1024]).then_inc(sem.qw01, 1)
+    te.wait_ge(sem.kc2, 1)
+    te.wait_ge(sem.kp2, 1)
+    te.wait_ge(sem.qw23, 1)
+    product(3, T.w3q, T.w3s, 0, C, 3, sem.m3)
+    te.wait_ge(sem.qx3, 1)
+    product(3, T.w3q, T.w3s, NEW, C, 4, sem.m3)
+    product(2, T.w3q, T.w3s, 0, C, 2, sem.m2)
+    te.wait_ge(sem.qw01, 1)
+    te.wait_ge(sem.kc1, 1)
+    te.wait_ge(sem.kp1, 1)
+    product(1, T.w2q, T.w2s, 0, C, 1, sem.m1)
+    te.wait_ge(sem.qa, 1)
+    product(0, T.a0q, T.a0s, 0, C, 0, sem.m0)
+    sc.wait_ge(sem.m3, 2)
+    sc.activation(T.yw[:, 0:C], T.ps[:, 512 * 3:512 * 3 + C], Copy).then_inc(sem.e3, 1)
+    sc.activation(T.yw[:, NEW:WIN], T.ps[:, 512 * 4:512 * 4 + C], Copy).then_inc(sem.e3, 1)
+    sc.wait_ge(sem.m2, 1)
+    sc.activation(T.yo[:, 2 * C:3 * C], T.ps[:, 1024:1024 + C], Copy).then_inc(sem.e2, 1)
+    for b in (1, 0):
+        v.wait_ge(sem["m%d" % b], 1)
+        v.tensor_copy(T.yo[:, C * b:C * b + C], T.ps[:, 512 * b:512 * b + C]).then_inc(sem["e%d" % b], 1)
     sy.wait_ge(sem.left3, left)
-    for b in (0, 1, 2):
+    for b in (2, 1, 0):
         sy.wait_ge(sem["e%d" % b], 1)
         sy.dma_start(T.y[:, C * b:C * b + C], T.yo[:, C * b:C * b + C]).then_inc(sem.stored, 16)
 

@@ -4,9 +4,12 @@ from concourse.mybir import dt, AluOpType, ActivationFunctionType
 C = 256
 CAP = 64
 LAND = 3 * CAP
-NEW = C + LAND
+NEW = C + 4 * CAP
 WIN = NEW + C
 F8, U8 = "float8_e4m3fn_x4", "uint8"
+GATES = {0: ["x2", "x3", "w3"], 1: ["w0"], 2: ["w1", "w2"]}
+LATE = ["w3", "w0", "x3", "w1", "w2"]
+NSC = 5
 
 SCRATCH = {
     "xb": ("sbuf", [128, 4096], "bfloat16"),
@@ -14,48 +17,41 @@ SCRATCH = {
     "a0q": ("sbuf", [128, C], F8), "a0s": ("sbuf", [128, C], U8),
     "wq": ("sbuf", [128, 512], F8), "ws": ("sbuf", [128, 512], U8),
     "sli": ("sbuf", [128, 48], "int32"), "pai": ("sbuf", [128, 48], "int32"),
-    "ipart": ("sbuf", [128, 1], "int32"), "icol": ("sbuf", [128, 48], "int32"),
-    "imod": ("sbuf", [128, LAND], "float32"), "irep": ("sbuf", [128, 16], "int32"),
-    "ibit": ("sbuf", [128, 2], "int32"), "fbit": ("sbuf", [128, 2], "float32"),
-    "jnew": ("sbuf", [128, 48], "int32"), "offrep": ("sbuf", [128, 16], "uint16"),
-    "mask": ("sbuf", [128, LAND], "float32"), "keep": ("sbuf", [128, LAND], "float32"),
-    "neg": ("sbuf", [128, 48], "int32"), "negj": ("sbuf", [128, 48], "int32"),
-    "high": ("sbuf", [128, 48], "int32"), "low": ("sbuf", [128, 48], "int32"),
+    "ipart": ("sbuf", [128, 1], "int32"), "irep": ("sbuf", [128, 34], "int32"), "icol": ("sbuf", [128, 48], "int32"),
+    "ibit": ("sbuf", [128, 3], "int32"), "fbit": ("sbuf", [128, 3], "float32"),
+    "jneg": ("sbuf", [128, 48], "float32"), "offrep": ("sbuf", [128, 16], "uint16"),
+    "offdup": ("sbuf", [128, 2], "uint16"), "offs": ("sbuf", [128, 16], "uint16"),
+    "dup": ("sbuf", [128, 32], "uint16"), "newp": ("sbuf", [128, 48], "float32"),
     "mf": ("sbuf", [128, 48], "float32"), "offm": ("sbuf", [128, 48], "uint16"),
-    "offs": ("sbuf", [128, 48], "uint16"),
     "yo": ("sbuf", [128, 1024], "float32"), "yw": ("sbuf", [128, WIN], "float32"),
-    "ps": ("psum", [128, 512 * 6], "float32"),
+    "ps": ("psum", [128, 512 * 7], "float32"),
 }
+SEMAPHORES = ["x0a", "x0b", "x1", "x2", "x3", "w0", "w1", "w2", "w3", "sl_in", "pa_in", "iop", "ior", "ioc", "vc", "cst",
+              "ofs", "om", "mf", "dup", "qa", "qx0", "qx1", "qx2", "qx3", "qw0", "qw1", "qw2", "qw3",
+              "kc1", "kc2", "kp1", "kp2", "m0", "m1", "m2", "m3", "m3n", "m3l", "m3m",
+              "e0", "e1", "e2", "e3", "e3l", "fin", "stored"]
 for _t in (1, 2, 3):
     SCRATCH["w%dq" % _t] = ("sbuf", [128, WIN], F8)
     SCRATCH["w%ds" % _t] = ("sbuf", [128, WIN], U8)
     SCRATCH["s%dq" % _t] = ("sbuf", [128, LAND], F8)
     SCRATCH["s%ds" % _t] = ("sbuf", [128, LAND], U8)
+    SEMAPHORES += [n % _t for n in ("pca%d", "pcb%d", "ppa%d", "ppb%d", "lc%d", "lp%d", "leftc%d", "leftp%d")]
     if _t > 1:
         SCRATCH["rg%d" % _t] = ("sbuf", [128, C], "float32")
         SCRATCH["tr%d" % _t] = ("sbuf", [128, C], "float32")
-        SCRATCH["gm%d" % _t] = ("sbuf", [128, LAND], "float32")
-        SCRATCH["sc%d" % _t] = ("sbuf", [128, LAND], "float32")
+        SCRATCH["gg%d" % _t] = ("sbuf", [128, LAND], "float32")
+        SCRATCH["gt%d" % _t] = ("sbuf", [128, LAND], "float32")
         SCRATCH["off%d" % _t] = ("sbuf", [128, 12], "uint16")
-
-SEMAPHORES = ["x0", "x1", "x2", "x3", "sl_in", "pa_in", "w01", "w23", "iot", "vc",
-              "ofs", "om", "mf", "rg2", "rg3", "l2", "l3", "qa", "qx0", "qx1", "qx2", "qx3", "qw01", "qw23",
-              "pc1", "pc2", "pc3", "pp1", "pp2", "pp3", "lc1", "lc2", "lc3", "lp1", "lp2", "lp3",
-              "left1", "left2", "left3", "kc1", "kc2", "kp1", "kp2",
-              "m0", "m1", "m2", "m3", "m3l", "e0", "e1", "e2", "e3", "e3l", "fin", "stored"]
+        SEMAPHORES += [n % _t for n in ("rg%d", "tr%d", "gg%d", "l%d")]
 
 
-def send_masks(core, ranks, topo):
+def send_calls(core, ranks, topo):
     def way(c):
         a, b = topo.chip(core), topo.chip(c)
         return 1 if topo.mates(a, b) else 2 if topo.same_plane(a, b) else 0
-    far = sorted([(way(c), s, c) for s, c in enumerate(ranks) if c != core])
-    eng = [e for e in topo.engines(core, far[0][2]) if all(e in topo.engines(core, c) for _, _, c in far)]
-    one, two = eng[0::2], eng[1::2]
-    h = len(one) // 2
-    codes = [one, two[:h], two[h:]]
-    plane = [one[:h], one[h:], two]
-    return [(s, codes[i], plane[i]) for i, (_, s, _) in enumerate(far)]
+    far, a, b = [s for _, s in sorted((way(c), s) for s, c in enumerate(ranks) if c != core)]
+    eng = [e for e in topo.engines(core, ranks[far]) if all(e in topo.engines(core, ranks[s]) for s in (a, b))]
+    return [[(far, eng)], [(a, eng[0::2]), (b, eng[1::2])]]
 
 
 def rank_program(g, core, T, topo):
@@ -65,23 +61,39 @@ def rank_program(g, core, T, topo):
     v, sc, te, sy, sem = g.vector, g.scalar, g.tensor, g.sync, T.sem
     Copy = ActivationFunctionType.Copy
     ranks = list(T.cores)
-    place = lambda owner, other: other if other < owner else other - 1
+    others = [d for d in range(len(ranks)) if d != r]
+    wire = send_calls(core, ranks, topo)
+    far, near = [d for d, _ in wire[0]], sorted(d for d, _ in wire[1])
+    at = lambda d: CAP * others.index(d)
 
-    sy.dma_start(T.xb[:, 0:1024], T.x[:, 0:1024]).then_inc(sem.x0, 16)
+    def spans(ds):
+        out = []
+        for d in ds:
+            if out and out[-1][1] == d:
+                out[-1][1] = d + 1
+            else:
+                out.append([d, d + 1])
+        return out
+
+    kept = spans(others)
+
+    def load(name):
+        k, (buf, src, n) = int(name[1]), ((T.xb, T.x, 1024) if name[0] == "x" else (T.wb, T.w, 512))
+        sy.dma_start(buf[:, n * k:n * k + n], src[:, n * k:n * k + n]).then_inc(sem[name], 16)
+
+    sy.dma_start(T.xb[:, 0:512], T.x[:, 0:512]).then_inc(sem.x0a, 16)
     for k in range(8):
-        q = sc if k < 6 else sy
+        q = sc if k < NSC else sy
         q.dma_start(T.sli[16 * k:16 * k + 16, :], T.sl[:]).then_inc(sem.sl_in, 16)
+    sy.dma_start(T.xb[:, 512:1024], T.x[:, 512:1024]).then_inc(sem.x0b, 16)
     for k in range(8):
         sy.dma_start(T.pai[16 * k:16 * k + 16, :], T.pa[:]).then_inc(sem.pa_in, 16)
-    sy.dma_start(T.xb[:, 1024:2048], T.x[:, 1024:2048]).then_inc(sem.x1, 16)
-    sy.dma_start(T.xb[:, 2048:3072], T.x[:, 2048:3072]).then_inc(sem.x2, 16)
-    sy.dma_start(T.xb[:, 3072:4096], T.x[:, 3072:4096]).then_inc(sem.x3, 16)
-    sy.dma_start(T.wb[:, 1024:2048], T.w[:, 1024:2048]).then_inc(sem.w23, 16)
+    for name in ["x1"] + GATES[0]:
+        load(name)
 
-    g.iota(T.ipart[:], [[0, 1]], 0, 1).then_inc(sem.iot, 1)
-    g.iota(T.irep[:], [[2, 8], [0, 2]], 0, 0).then_inc(sem.iot, 1)
-    g.iota(T.icol[:], [[0, 3], [16, 16]], NEW, 0).then_inc(sem.iot, 1)
-    g.iota(T.imod[:], [[0, 12], [1, 16]], 0, 0, allow_small_or_imprecise_dtypes=True).then_inc(sem.iot, 1)
+    g.iota(T.ipart[:], [[0, 1]], 0, 1).then_inc(sem.iop, 1)
+    g.iota(T.irep[:], [[2, 17], [0, 2]], 0, 0).then_inc(sem.ior, 1)
+    g.iota(T.icol[:], [[0, 3], [-16, 16]], -NEW, 0).then_inc(sem.ioc, 1)
 
     nv = [0]
 
@@ -92,175 +104,194 @@ def rank_program(g, core, T, topo):
     def settle():
         v.wait_ge(sem.vc, nv[0])
 
-    v.wait_ge(sem.iot, 4)
+    v.wait_ge(sem.iop, 1)
     chain(v.tensor_scalar(T.ibit[:, 0:1], T.ipart[:], 15, None, AluOpType.bitwise_and))
     chain(v.tensor_scalar(T.ibit[:, 1:2], T.ipart[:], 4, 1, AluOpType.arith_shift_right, AluOpType.bitwise_and))
+    chain(v.tensor_scalar(T.ibit[:, 2:3], T.ipart[:], 14, None, AluOpType.bitwise_and))
     settle()
     chain(v.tensor_copy(T.fbit[:], T.ibit[:]))
-    chain(v.tensor_scalar(T.keep[:], T.imod[:], 0.0, None, AluOpType.not_equal))
     settle()
-    chain(v.tensor_scalar(T.jnew[:], T.icol[:], T.fbit[:, 0:1], None, AluOpType.add))
-    chain(v.tensor_scalar(T.offrep[:], T.irep[:], T.fbit[:, 1:2], None, AluOpType.add))
-    chain(v.tensor_scalar(T.mask[:], T.imod[:], T.fbit[:, 0:1], None, AluOpType.is_equal))
+    v.wait_ge(sem.ior, 1)
+    chain(v.tensor_scalar(T.offdup[:], T.irep[:, 16:33:16], T.fbit[:, 2:3], T.fbit[:, 1:2], AluOpType.add, AluOpType.add))
+    v.tensor_scalar(T.offrep[:], T.irep[:, 0:16], T.fbit[:, 1:2], None, AluOpType.add).then_inc(sem.cst, 1)
+    v.wait_ge(sem.ioc, 1)
+    chain(v.tensor_scalar(T.jneg[:], T.icol[:], T.fbit[:, 0:1], None, AluOpType.subtract))
 
-    runs = [(a, b, o) for a, b, o in ((0, 4 * r, 0), (4 * r + 4, 16, 4 * r)) if b > a]
-
+    v.wait_ge(sem.x0a, 16)
+    v.quantize_mx(T.a0q[:, 0:128], T.a0s[:, 0:128], T.xb[:, 0:512]).then_inc(sem.qa, 1)
     v.wait_ge(sem.sl_in, 128)
-    v.tensor_copy(T.offs[:], T.sli[:]).then_inc(sem.ofs, 1)
-    v.wait_ge(sem.x0, 16)
-    v.quantize_mx(T.a0q[:], T.a0s[:], T.xb[:, 0:1024]).then_inc(sem.qa, 1)
-    v.wait_ge(sem.ofs, 1)
-    v.wait_ge(sem.qa, 1)
-    sc.wait_ge(sem.ofs, 1)
-    sc.wait_ge(sem.qa, 1)
-    for a, b, o in runs:
-        m, n = 16 * o, 16 * (o + b - a)
-        v.tensor_copy(T.s1q[:, m:n].bitcast(dt.uint32),
-                      T.a0q[:].bitcast(dt.uint32).indirect(T.offs[:, a:b])).then_inc(sem.pc1, 1)
-        sc.activation(T.s1s[:, m:n], T.a0s[:].indirect(T.offs[:, a:b]), Copy).then_inc(sem.pp1, 1)
+    v.tensor_copy(T.offs[:], T.sli[:, 0:16]).then_inc(sem.ofs, 1)
+    v.wait_ge(sem.x0b, 16)
+    v.quantize_mx(T.a0q[:, 128:C], T.a0s[:, 128:C], T.xb[:, 512:1024]).then_inc(sem.qa, 1)
+    settle()
+    for q in (v, sc):
+        q.wait_ge(sem.ofs, 1)
+        q.wait_ge(sem.qa, 2)
 
-    plan = send_masks(core, ranks, topo)
+    def pick(t, wq, ws, off, col):
+        n = []
+        for ds, k in ((far, "a"), (near, "b")):
+            for d, e in spans(ds):
+                a, b, i, j = at(d), at(d) + CAP * (e - d), col(d), col(d) + 4 * (e - d)
+                v.tensor_copy(T["s%dq" % t][:, a:b].bitcast(dt.uint32),
+                              wq[:].bitcast(dt.uint32).indirect(off[:, i:j])).then_inc(sem["pc%s%d" % (k, t)], 1)
+                sc.activation(T["s%ds" % t][:, a:b], ws[:].indirect(off[:, i:j]), Copy).then_inc(sem["pp%s%d" % (k, t)], 1)
+            n.append(len(spans(ds)))
+        return n
+
     bits = lambda es: sum(1 << e for e in es)
-    got_c, got_p = 0, 0
-    for s, c in enumerate(ranks):
-        if c != core:
-            for d, ec, ep in send_masks(c, ranks, topo):
-                if d == r:
-                    got_c += len(ec)
-                    got_p += len(ep)
-    left = sum(len(p[1]) + len(p[2]) for p in plan)
+    got = sum(len(es) for s, c in enumerate(ranks) if s != r for k in send_calls(c, ranks, topo) for d, es in k if d == r)
+    left = sum(len(es) for k in wire for d, es in k)
 
-    def send(t, n_picks):
-        for part in (0, 1):
-            g.wait_ge(sem["pp%d" % t] if part else sem["pc%d" % t], n_picks)
-            moves = []
-            for d, ec, ep in plan:
-                rid, pid, _ = topo.addr(ranks[d])
-                a, b = CAP * place(r, d), C + CAP * place(d, r)
-                if part:
-                    src, dst = T["s%ds" % t][:, a:a + CAP], T["w%ds" % t][:, b:b + CAP]
-                else:
-                    src = T["s%dq" % t][:, a:a + CAP].bitcast(dt.uint8)
-                    dst = T["w%dq" % t][:, b:b + CAP].bitcast(dt.uint8)
-                moves.append(RemoteDMATransfer(dst_ids=[DstId(rid=rid, pnc=pid)], dma_engine_mask=bits(ep if part else ec),
-                                               remote_sem=sem["lp%d" % t] if part else sem["lc%d" % t],
-                                               src=src, dst=dst))
-            g.remote_dma_fused(moves, local_sem=sem["left%d" % t])
+    def send(t, picks):
+        for part in ("c", "p"):
+            for moves, k, n in zip(wire, "ab", picks):
+                g.wait_ge(sem["p%s%s%d" % (part, k, t)], n)
+                transfers = []
+                for d, es in moves:
+                    rid, pid, _ = topo.addr(ranks[d])
+                    a, b = at(d), C + CAP * r
+                    if part == "c":
+                        src = T["s%dq" % t][:, a:a + CAP].bitcast(dt.uint8)
+                        dst = T["w%dq" % t][:, b:b + CAP].bitcast(dt.uint8)
+                    else:
+                        src, dst = T["s%ds" % t][:, a:a + CAP], T["w%ds" % t][:, b:b + CAP]
+                    transfers.append(RemoteDMATransfer(dst_ids=[DstId(rid=rid, pnc=pid)], dma_engine_mask=bits(es),
+                                                       remote_sem=sem["l%s%d" % (part, t)], src=src, dst=dst))
+                g.remote_dma_fused(transfers, local_sem=sem["left%s%d" % (part, t)])
 
-    send(1, len(runs))
+    send(1, pick(1, T.a0q, T.a0s, T.offs, lambda d: 4 * d))
 
+    v.tensor_copy(T.dup[:], T.sli[:].indirect(T.offdup[:, 0:2])).then_inc(sem.dup, 1)
     v.wait_ge(sem.pa_in, 128)
-    chain(v.tensor_scalar(T.neg[:], T.pai[:], 0, None, AluOpType.is_lt))
-    if r < 3:
-        chain(v.tensor_scalar(T.high[:], T.pai[:], C + CAP * (r + 1), -CAP, AluOpType.is_ge, AluOpType.mult))
+    chain(v.tensor_tensor(T.newp[:], T.pai[:], T.jneg[:], AluOpType.mult))
     settle()
-    chain(v.tensor_tensor(T.negj[:], T.neg[:], T.jnew[:], AluOpType.mult))
-    low = T.pai
-    if r < 3:
-        chain(v.tensor_tensor(T.low[:], T.pai[:], T.high[:], AluOpType.add))
-        low = T.low
-    settle()
-    v.tensor_tensor(T.mf[:], low[:], T.negj[:], AluOpType.max).then_inc(sem.mf, 1)
-    sc.wait_ge(sem.mf, 1)
-    for t in (2, 3):
-        a = 16 * (t - 2)
-        sc.activation(T["rg%d" % t][:], T.mf[:, a:a + 16].indirect(T.offrep[:, 0:16]), Copy).then_inc(sem["rg%d" % t], 1)
-
-    def compose(t):
-        tr, gm, ss, off = T["tr%d" % t], T["gm%d" % t], T["sc%d" % t], T["off%d" % t]
-        v.wait_ge(sem["rg%d" % t], 1)
-        chain(v.transpose(tr[:], T["rg%d" % t][:]))
-        settle()
-        for a, b, o in runs:
-            m, n, c = 16 * o, 16 * (o + b - a), 16 * (t - 1)
-            chain(v.tensor_tensor(gm[:, m:n], tr[:].indirect(T.offs[:, c + a:c + b]), T.mask[:, m:n], AluOpType.mult))
-        settle()
-        chain(v.tensor_tensor_scan(ss[:], T.keep[:], gm[:], 0.0, AluOpType.mult, AluOpType.add))
-        settle()
-        v.tensor_copy(off[:], ss[:, 15:LAND:16]).then_inc(sem["l%d" % t], 1)
-
+    v.tensor_tensor(T.mf[:], T.pai[:], T.newp[:], AluOpType.max).then_inc(sem.mf, 1)
     v.quantize_mx(T.w1q[:, 0:C], T.w1s[:, 0:C], T.xb[:, 0:1024]).then_inc(sem.qx0, 1)
     v.wait_ge(sem.mf, 1)
     v.tensor_copy(T.offm[:], T.mf[:]).then_inc(sem.om, 1)
-    compose(2)
+
+    def repeat(t):
+        a = 16 * (t - 2)
+        sc.activation(T["rg%d" % t][:], T.mf[:, a:a + 16].indirect(T.offrep[:, 0:16]), Copy).then_inc(sem["rg%d" % t], 1)
+
+    def flatten(t):
+        v.wait_ge(sem["rg%d" % t], 1)
+        v.transpose(T["tr%d" % t][:], T["rg%d" % t][:]).then_inc(sem["tr%d" % t], 1)
+
+    def through(t):
+        sc.wait_ge(sem["tr%d" % t], 1)
+        for d, e in kept:
+            a, b = at(d), 16 * (t - 2)
+            sc.activation(T["gg%d" % t][:, a:a + CAP * (e - d)], T["tr%d" % t][:].indirect(T.dup[:, b + 4 * d:b + 4 * e]),
+                          Copy).then_inc(sem["gg%d" % t], 1)
+
+    def wrap(t):
+        v.wait_ge(sem["gg%d" % t], len(kept))
+        chain(v.transpose(T["gt%d" % t][:], T["gg%d" % t][:]))
+        settle()
+        v.tensor_copy(T["off%d" % t][:], T["gt%d" % t][:, 0:LAND:16]).then_inc(sem["l%d" % t], 1)
+
+    sc.wait_ge(sem.cst, 1)
+    sc.wait_ge(sem.mf, 1)
+    repeat(2)
+    flatten(2)
+    sc.wait_ge(sem.dup, 1)
+    through(2)
+    repeat(3)
     v.wait_ge(sem.x1, 16)
     v.quantize_mx(T.w1q[:, NEW:WIN], T.w1s[:, NEW:WIN], T.xb[:, 1024:2048]).then_inc(sem.qx1, 1)
+    wrap(2)
 
-    sy.wait_ge(sem.left1, left)
-    sy.wait_ge(sem.left2, left)
-    sy.dma_start(T.wb[:, 0:1024], T.w[:, 0:1024]).then_inc(sem.w01, 16)
+    for t in (1, 2):
+        sy.wait_ge(sem["leftc%d" % t], left)
+        for name in GATES[t]:
+            load(name)
+
+    for t in (2, 3):
+        u = t - 1
+        wq, ws, off = T["w%dq" % u], T["w%ds" % u], T["off%d" % t]
+        for q, own, landed in ((v, "c", "lc%d"), (sc, "p", "lp%d")):
+            q.wait_ge(sem.qx0 if t == 2 else sem["k%s1" % own], 1)
+            q.wait_ge(sem["qx%d" % u], 1)
+            q.wait_ge(sem["l%d" % t], 1)
+            q.wait_ge(sem[landed % u], got)
+        send(t, pick(t, wq, ws, off, lambda d: at(d) // 16))
+        kq, ks, om = T["w%dq" % t], T["w%ds" % t], T.offm[:, 16 * (t - 2):16 * (t - 1)]
+        v.wait_ge(sem.om, 1)
+        v.tensor_copy(kq[:, 0:C].bitcast(dt.uint32), wq[:].bitcast(dt.uint32).indirect(om)).then_inc(sem["kc%d" % u], 1)
+        sc.wait_ge(sem.om, 1)
+        if t == 2:
+            flatten(3)
+            through(3)
+        sc.activation(ks[:, 0:C], ws[:].indirect(om), Copy).then_inc(sem["kp%d" % u], 1)
+        if t == 2:
+            v.wait_ge(sem.x2, 16)
+            v.quantize_mx(T.w2q[:, NEW:WIN], T.w2s[:, NEW:WIN], T.xb[:, 2048:3072]).then_inc(sem.qx2, 1)
+            wrap(3)
+
+    for name in LATE:
+        k = int(name[1])
+        v.wait_ge(sem[name], 16)
+        if name[0] == "w":
+            v.quantize_mx(T.wq[:, 128 * k:128 * k + 128], T.ws[:, 128 * k:128 * k + 128],
+                          T.wb[:, 512 * k:512 * k + 512]).then_inc(sem["qw%d" % k], 1)
+        else:
+            v.quantize_mx(T.w3q[:, NEW:WIN], T.w3s[:, NEW:WIN], T.xb[:, 3072:4096]).then_inc(sem.qx3, 1)
 
     def product(t, src, ssrc, a, n, bank, done):
         te.matmul_mx(T.ps[:, 512 * bank:512 * bank + n], T.wq[:, 128 * t:128 * t + 128], T.ws[:, 128 * t:128 * t + 128],
                      src[:, a:a + n], ssrc[:, a:a + n], True, True).then_inc(done, 1)
 
-    for t in (2, 3):
-        wq, ws = T["w%dq" % (t - 1)], T["w%ds" % (t - 1)]
-        sq, ss = T["s%dq" % t], T["s%ds" % t]
-        off, u = T["off%d" % t], t - 1
-        v.wait_ge(sem.qx0 if t == 2 else sem.kc1, 1)
-        sc.wait_ge(sem.qx0 if t == 2 else sem.kp1, 1)
-        for q, landed, n in ((v, sem["lc%d" % u], got_c), (sc, sem["lp%d" % u], got_p)):
-            q.wait_ge(sem.qx1 if t == 2 else sem.qx2, 1)
-            q.wait_ge(sem["l%d" % t], 1)
-            q.wait_ge(landed, n)
-        v.tensor_copy(sq[:].bitcast(dt.uint32), wq[:].bitcast(dt.uint32).indirect(off[:, 0:12])).then_inc(sem["pc%d" % t], 1)
-        sc.activation(ss[:], ws[:].indirect(off[:, 0:12]), Copy).then_inc(sem["pp%d" % t], 1)
-        send(t, 1)
-        kq, ks = T["w%dq" % t], T["w%ds" % t]
-        om = T.offm[:, 16 * (t - 2):16 * (t - 1)]
-        v.wait_ge(sem.om, 1)
-        v.tensor_copy(kq[:, 0:C].bitcast(dt.uint32), wq[:].bitcast(dt.uint32).indirect(om)).then_inc(sem["kc%d" % u], 1)
-        sc.wait_ge(sem.om, 1)
-        sc.activation(ks[:, 0:C], ws[:].indirect(om), Copy).then_inc(sem["kp%d" % u], 1)
-        if t == 2:
-            compose(3)
-            v.wait_ge(sem.x2, 16)
-            v.quantize_mx(T.w2q[:, NEW:WIN], T.w2s[:, NEW:WIN], T.xb[:, 2048:3072]).then_inc(sem.qx2, 1)
+    def ready(*names):
+        for n in names:
+            te.wait_ge(sem[n], 1)
 
-    v.wait_ge(sem.w23, 16)
-    v.quantize_mx(T.wq[:, 256:512], T.ws[:, 256:512], T.wb[:, 1024:2048]).then_inc(sem.qw23, 1)
-    v.wait_ge(sem.x3, 16)
-    v.quantize_mx(T.w3q[:, NEW:WIN], T.w3s[:, NEW:WIN], T.xb[:, 3072:4096]).then_inc(sem.qx3, 1)
-    v.wait_ge(sem.w01, 16)
-    v.quantize_mx(T.wq[:, 0:256], T.ws[:, 0:256], T.wb[:, 0:1024]).then_inc(sem.qw01, 1)
-    te.wait_ge(sem.kc2, 1)
-    te.wait_ge(sem.kp2, 1)
-    te.wait_ge(sem.qw23, 1)
-    product(3, T.w3q, T.w3s, 0, C, 3, sem.m3)
-    te.wait_ge(sem.qx3, 1)
-    product(3, T.w3q, T.w3s, NEW, C, 4, sem.m3)
-    product(2, T.w3q, T.w3s, 0, C, 2, sem.m2)
-    te.wait_ge(sem.qw01, 1)
-    te.wait_ge(sem.kc1, 1)
-    te.wait_ge(sem.kp1, 1)
-    product(1, T.w2q, T.w2s, 0, C, 1, sem.m1)
-    te.wait_ge(sem.qa, 1)
+    te.wait_ge(sem.qa, 2)
+    ready("qw0")
     product(0, T.a0q, T.a0s, 0, C, 0, sem.m0)
-    sc.wait_ge(sem.m3, 2)
+    ready("qw3", "qx3")
+    product(3, T.w3q, T.w3s, NEW, C, 4, sem.m3n)
+    ready("qw1", "kc1", "kp1")
+    product(1, T.w2q, T.w2s, 0, C, 1, sem.m1)
+    ready("kc2", "kp2")
+    product(3, T.w3q, T.w3s, 0, C, 3, sem.m3)
+    ready("qw2")
+    product(2, T.w3q, T.w3s, 0, C, 2, sem.m2)
+    for b in (0, 1):
+        sc.wait_ge(sem["m%d" % b], 1)
+        sc.activation(T.yo[:, C * b:C * b + C], T.ps[:, 512 * b:512 * b + C], Copy).then_inc(sem["e%d" % b], 1)
+    sc.wait_ge(sem.m3, 1)
     sc.activation(T.yw[:, 0:C], T.ps[:, 512 * 3:512 * 3 + C], Copy).then_inc(sem.e3, 1)
-    sc.activation(T.yw[:, NEW:WIN], T.ps[:, 512 * 4:512 * 4 + C], Copy).then_inc(sem.e3, 1)
-    sc.wait_ge(sem.m2, 1)
-    sc.activation(T.yo[:, 2 * C:3 * C], T.ps[:, 1024:1024 + C], Copy).then_inc(sem.e2, 1)
-    for b in (1, 0):
-        v.wait_ge(sem["m%d" % b], 1)
-        v.tensor_copy(T.yo[:, C * b:C * b + C], T.ps[:, 512 * b:512 * b + C]).then_inc(sem["e%d" % b], 1)
-    sy.wait_ge(sem.left3, left)
-    for b in (2, 1, 0):
+    v.wait_ge(sem.m3n, 1)
+    v.tensor_copy(T.yw[:, NEW:WIN], T.ps[:, 512 * 4:512 * 4 + C]).then_inc(sem.e3, 1)
+    v.wait_ge(sem.m2, 1)
+    v.tensor_copy(T.yo[:, 2 * C:3 * C], T.ps[:, 512 * 2:512 * 2 + C]).then_inc(sem.e2, 1)
+    sy.wait_ge(sem.leftc3, left)
+    for b in (0, 1, 2):
         sy.wait_ge(sem["e%d" % b], 1)
         sy.dma_start(T.y[:, C * b:C * b + C], T.yo[:, C * b:C * b + C]).then_inc(sem.stored, 16)
 
-    te.wait_ge(sem.lc3, got_c)
-    te.wait_ge(sem.lp3, got_p)
-    product(3, T.w3q, T.w3s, C, LAND, 5, sem.m3l)
-    v.wait_ge(sem.m3l, 1)
-    v.tensor_copy(T.yw[:, C:NEW], T.ps[:, 512 * 5:512 * 5 + LAND]).then_inc(sem.e3l, 1)
-    v.wait_ge(sem.e3, 2)
-    v.wait_ge(sem.e3l, 1)
+    te.wait_ge(sem.lc3, got)
+    te.wait_ge(sem.lp3, got)
+    for i, (d, e) in enumerate(kept):
+        a, n = C + CAP * d, max(128, CAP * (e - d))
+        skip = CAP if CAP * (e - d) < 128 and d == 0 else 0
+        product(3, T.w3q, T.w3s, a - skip, n, 5 + i, sem.m3m if i else sem.m3l)
+        src, dst = T.ps[:, 512 * (5 + i) + skip:512 * (5 + i) + skip + CAP * (e - d)], T.yw[:, a:C + CAP * e]
+        if i:
+            sc.wait_ge(sem.m3m, 1)
+            sc.activation(dst, src, Copy).then_inc(sem.e3l, 1)
+        else:
+            v.wait_ge(sem.m3l, 1)
+            v.tensor_copy(dst, src).then_inc(sem.e3l, 1)
+    for q in (v, sc):
+        q.wait_ge(sem.e3, 2)
+        q.wait_ge(sem.e3l, len(kept))
     v.tensor_copy(T.yo[:, 3 * C + 128:4 * C], T.yw[:].indirect(T.offm[:, 40:48])).then_inc(sem.fin, 1)
-    sc.wait_ge(sem.e3, 2)
-    sc.wait_ge(sem.e3l, 1)
     sc.activation(T.yo[:, 3 * C:3 * C + 128], T.yw[:].indirect(T.offm[:, 32:40]), Copy).then_inc(sem.fin, 1)
     sy.wait_ge(sem.fin, 2)
     sy.dma_start(T.y[:, 3 * C:4 * C], T.yo[:, 3 * C:4 * C]).then_inc(sem.stored, 16)
+    for t in (1, 2, 3):
+        sy.wait_ge(sem["leftp%d" % t], left)
     sy.wait_ge(sem.stored, 64)

from concourse.bass import DstId, RemoteDMATransfer
from concourse.mybir import dt, AluOpType, ActivationFunctionType

C = 256
CAP = 64
LAND = 3 * CAP
NEW = C + 4 * CAP
WIN = NEW + C
F8, U8 = "float8_e4m3fn_x4", "uint8"
GATES = {0: ["x2", "x3", "w3"], 1: ["w0"], 2: ["w1", "w2"]}
LATE = ["w3", "w0", "x3", "w1", "w2"]
NSC = 5

SCRATCH = {
    "xb": ("sbuf", [128, 4096], "bfloat16"),
    "wb": ("sbuf", [128, 2048], "bfloat16"),
    "a0q": ("sbuf", [128, C], F8), "a0s": ("sbuf", [128, C], U8),
    "wq": ("sbuf", [128, 512], F8), "ws": ("sbuf", [128, 512], U8),
    "sli": ("sbuf", [128, 48], "int32"), "pai": ("sbuf", [128, 48], "int32"),
    "ipart": ("sbuf", [128, 1], "int32"), "irep": ("sbuf", [128, 34], "int32"), "icol": ("sbuf", [128, 48], "int32"),
    "ibit": ("sbuf", [128, 3], "int32"), "fbit": ("sbuf", [128, 3], "float32"),
    "jneg": ("sbuf", [128, 48], "float32"), "offrep": ("sbuf", [128, 16], "uint16"),
    "offdup": ("sbuf", [128, 2], "uint16"), "offs": ("sbuf", [128, 16], "uint16"),
    "dup": ("sbuf", [128, 32], "uint16"), "newp": ("sbuf", [128, 48], "float32"),
    "mf": ("sbuf", [128, 48], "float32"), "offm": ("sbuf", [128, 48], "uint16"),
    "yo": ("sbuf", [128, 1024], "float32"), "yw": ("sbuf", [128, WIN], "float32"),
    "ps": ("psum", [128, 512 * 7], "float32"),
}
SEMAPHORES = ["x0a", "x0b", "x1", "x2", "x3", "w0", "w1", "w2", "w3", "sl_in", "pa_in", "iop", "ior", "ioc", "vc", "cst",
              "ofs", "om", "mf", "dup", "qa", "qx0", "qx1", "qx2", "qx3", "qw0", "qw1", "qw2", "qw3",
              "kc1", "kc2", "kp1", "kp2", "m0", "m1", "m2", "m3", "m3n", "m3l", "m3m",
              "e0", "e1", "e2", "e3", "e3l", "fin", "stored"]
for _t in (1, 2, 3):
    SCRATCH["w%dq" % _t] = ("sbuf", [128, WIN], F8)
    SCRATCH["w%ds" % _t] = ("sbuf", [128, WIN], U8)
    SCRATCH["s%dq" % _t] = ("sbuf", [128, LAND], F8)
    SCRATCH["s%ds" % _t] = ("sbuf", [128, LAND], U8)
    SEMAPHORES += [n % _t for n in ("pca%d", "pcb%d", "ppa%d", "ppb%d", "lc%d", "lp%d", "leftc%d", "leftp%d")]
    if _t > 1:
        SCRATCH["rg%d" % _t] = ("sbuf", [128, C], "float32")
        SCRATCH["tr%d" % _t] = ("sbuf", [128, C], "float32")
        SCRATCH["gg%d" % _t] = ("sbuf", [128, LAND], "float32")
        SCRATCH["gt%d" % _t] = ("sbuf", [128, LAND], "float32")
        SCRATCH["off%d" % _t] = ("sbuf", [128, 12], "uint16")
        SEMAPHORES += [n % _t for n in ("rg%d", "tr%d", "gg%d", "l%d")]


def send_calls(core, ranks, topo):
    def way(c):
        a, b = topo.chip(core), topo.chip(c)
        return 1 if topo.mates(a, b) else 2 if topo.same_plane(a, b) else 0
    far, a, b = [s for _, s in sorted((way(c), s) for s, c in enumerate(ranks) if c != core)]
    eng = [e for e in topo.engines(core, ranks[far]) if all(e in topo.engines(core, ranks[s]) for s in (a, b))]
    return [[(far, eng)], [(a, eng[0::2]), (b, eng[1::2])]]


def rank_program(g, core, T, topo):
    r = T.rank_of(core)
    if r is None:
        return
    v, sc, te, sy, sem = g.vector, g.scalar, g.tensor, g.sync, T.sem
    Copy = ActivationFunctionType.Copy
    ranks = list(T.cores)
    others = [d for d in range(len(ranks)) if d != r]
    wire = send_calls(core, ranks, topo)
    far, near = [d for d, _ in wire[0]], sorted(d for d, _ in wire[1])
    at = lambda d: CAP * others.index(d)

    def spans(ds):
        out = []
        for d in ds:
            if out and out[-1][1] == d:
                out[-1][1] = d + 1
            else:
                out.append([d, d + 1])
        return out

    kept = spans(others)

    def load(name):
        k, (buf, src, n) = int(name[1]), ((T.xb, T.x, 1024) if name[0] == "x" else (T.wb, T.w, 512))
        sy.dma_start(buf[:, n * k:n * k + n], src[:, n * k:n * k + n]).then_inc(sem[name], 16)

    sy.dma_start(T.xb[:, 0:512], T.x[:, 0:512]).then_inc(sem.x0a, 16)
    for k in range(8):
        q = sc if k < NSC else sy
        q.dma_start(T.sli[16 * k:16 * k + 16, :], T.sl[:]).then_inc(sem.sl_in, 16)
    sy.dma_start(T.xb[:, 512:1024], T.x[:, 512:1024]).then_inc(sem.x0b, 16)
    for k in range(8):
        sy.dma_start(T.pai[16 * k:16 * k + 16, :], T.pa[:]).then_inc(sem.pa_in, 16)
    for name in ["x1"] + GATES[0]:
        load(name)

    g.iota(T.ipart[:], [[0, 1]], 0, 1).then_inc(sem.iop, 1)
    g.iota(T.irep[:], [[2, 17], [0, 2]], 0, 0).then_inc(sem.ior, 1)
    g.iota(T.icol[:], [[0, 3], [-16, 16]], -NEW, 0).then_inc(sem.ioc, 1)

    nv = [0]

    def chain(ins):
        ins.then_inc(sem.vc, 1)
        nv[0] += 1

    def settle():
        v.wait_ge(sem.vc, nv[0])

    v.wait_ge(sem.iop, 1)
    chain(v.tensor_scalar(T.ibit[:, 0:1], T.ipart[:], 15, None, AluOpType.bitwise_and))
    chain(v.tensor_scalar(T.ibit[:, 1:2], T.ipart[:], 4, 1, AluOpType.arith_shift_right, AluOpType.bitwise_and))
    chain(v.tensor_scalar(T.ibit[:, 2:3], T.ipart[:], 14, None, AluOpType.bitwise_and))
    settle()
    chain(v.tensor_copy(T.fbit[:], T.ibit[:]))
    settle()
    v.wait_ge(sem.ior, 1)
    chain(v.tensor_scalar(T.offdup[:], T.irep[:, 16:33:16], T.fbit[:, 2:3], T.fbit[:, 1:2], AluOpType.add, AluOpType.add))
    v.tensor_scalar(T.offrep[:], T.irep[:, 0:16], T.fbit[:, 1:2], None, AluOpType.add).then_inc(sem.cst, 1)
    v.wait_ge(sem.ioc, 1)
    chain(v.tensor_scalar(T.jneg[:], T.icol[:], T.fbit[:, 0:1], None, AluOpType.subtract))

    v.wait_ge(sem.x0a, 16)
    v.quantize_mx(T.a0q[:, 0:128], T.a0s[:, 0:128], T.xb[:, 0:512]).then_inc(sem.qa, 1)
    v.wait_ge(sem.sl_in, 128)
    v.tensor_copy(T.offs[:], T.sli[:, 0:16]).then_inc(sem.ofs, 1)
    v.wait_ge(sem.x0b, 16)
    v.quantize_mx(T.a0q[:, 128:C], T.a0s[:, 128:C], T.xb[:, 512:1024]).then_inc(sem.qa, 1)
    settle()
    for q in (v, sc):
        q.wait_ge(sem.ofs, 1)
        q.wait_ge(sem.qa, 2)

    def pick(t, wq, ws, off, col):
        n = []
        for ds, k in ((far, "a"), (near, "b")):
            for d, e in spans(ds):
                a, b, i, j = at(d), at(d) + CAP * (e - d), col(d), col(d) + 4 * (e - d)
                v.tensor_copy(T["s%dq" % t][:, a:b].bitcast(dt.uint32),
                              wq[:].bitcast(dt.uint32).indirect(off[:, i:j])).then_inc(sem["pc%s%d" % (k, t)], 1)
                sc.activation(T["s%ds" % t][:, a:b], ws[:].indirect(off[:, i:j]), Copy).then_inc(sem["pp%s%d" % (k, t)], 1)
            n.append(len(spans(ds)))
        return n

    bits = lambda es: sum(1 << e for e in es)
    got = sum(len(es) for s, c in enumerate(ranks) if s != r for k in send_calls(c, ranks, topo) for d, es in k if d == r)
    left = sum(len(es) for k in wire for d, es in k)

    def send(t, picks):
        for part in ("c", "p"):
            for moves, k, n in zip(wire, "ab", picks):
                g.wait_ge(sem["p%s%s%d" % (part, k, t)], n)
                transfers = []
                for d, es in moves:
                    rid, pid, _ = topo.addr(ranks[d])
                    a, b = at(d), C + CAP * r
                    if part == "c":
                        src = T["s%dq" % t][:, a:a + CAP].bitcast(dt.uint8)
                        dst = T["w%dq" % t][:, b:b + CAP].bitcast(dt.uint8)
                    else:
                        src, dst = T["s%ds" % t][:, a:a + CAP], T["w%ds" % t][:, b:b + CAP]
                    transfers.append(RemoteDMATransfer(dst_ids=[DstId(rid=rid, pnc=pid)], dma_engine_mask=bits(es),
                                                       remote_sem=sem["l%s%d" % (part, t)], src=src, dst=dst))
                g.remote_dma_fused(transfers, local_sem=sem["left%s%d" % (part, t)])

    send(1, pick(1, T.a0q, T.a0s, T.offs, lambda d: 4 * d))

    v.tensor_copy(T.dup[:], T.sli[:].indirect(T.offdup[:, 0:2])).then_inc(sem.dup, 1)
    v.wait_ge(sem.pa_in, 128)
    chain(v.tensor_tensor(T.newp[:], T.pai[:], T.jneg[:], AluOpType.mult))
    settle()
    v.tensor_tensor(T.mf[:], T.pai[:], T.newp[:], AluOpType.max).then_inc(sem.mf, 1)
    v.quantize_mx(T.w1q[:, 0:C], T.w1s[:, 0:C], T.xb[:, 0:1024]).then_inc(sem.qx0, 1)
    v.wait_ge(sem.mf, 1)
    v.tensor_copy(T.offm[:], T.mf[:]).then_inc(sem.om, 1)

    def repeat(t):
        a = 16 * (t - 2)
        sc.activation(T["rg%d" % t][:], T.mf[:, a:a + 16].indirect(T.offrep[:, 0:16]), Copy).then_inc(sem["rg%d" % t], 1)

    def flatten(t):
        v.wait_ge(sem["rg%d" % t], 1)
        v.transpose(T["tr%d" % t][:], T["rg%d" % t][:]).then_inc(sem["tr%d" % t], 1)

    def through(t):
        sc.wait_ge(sem["tr%d" % t], 1)
        for d, e in kept:
            a, b = at(d), 16 * (t - 2)
            sc.activation(T["gg%d" % t][:, a:a + CAP * (e - d)], T["tr%d" % t][:].indirect(T.dup[:, b + 4 * d:b + 4 * e]),
                          Copy).then_inc(sem["gg%d" % t], 1)

    def wrap(t):
        v.wait_ge(sem["gg%d" % t], len(kept))
        chain(v.transpose(T["gt%d" % t][:], T["gg%d" % t][:]))
        settle()
        v.tensor_copy(T["off%d" % t][:], T["gt%d" % t][:, 0:LAND:16]).then_inc(sem["l%d" % t], 1)

    sc.wait_ge(sem.cst, 1)
    sc.wait_ge(sem.mf, 1)
    repeat(2)
    flatten(2)
    sc.wait_ge(sem.dup, 1)
    through(2)
    repeat(3)
    v.wait_ge(sem.x1, 16)
    v.quantize_mx(T.w1q[:, NEW:WIN], T.w1s[:, NEW:WIN], T.xb[:, 1024:2048]).then_inc(sem.qx1, 1)
    wrap(2)

    for t in (1, 2):
        sy.wait_ge(sem["leftc%d" % t], left)
        for name in GATES[t]:
            load(name)

    for t in (2, 3):
        u = t - 1
        wq, ws, off = T["w%dq" % u], T["w%ds" % u], T["off%d" % t]
        for q, own, landed in ((v, "c", "lc%d"), (sc, "p", "lp%d")):
            q.wait_ge(sem.qx0 if t == 2 else sem["k%s1" % own], 1)
            q.wait_ge(sem["qx%d" % u], 1)
            q.wait_ge(sem["l%d" % t], 1)
            q.wait_ge(sem[landed % u], got)
        send(t, pick(t, wq, ws, off, lambda d: at(d) // 16))
        kq, ks, om = T["w%dq" % t], T["w%ds" % t], T.offm[:, 16 * (t - 2):16 * (t - 1)]
        v.wait_ge(sem.om, 1)
        v.tensor_copy(kq[:, 0:C].bitcast(dt.uint32), wq[:].bitcast(dt.uint32).indirect(om)).then_inc(sem["kc%d" % u], 1)
        sc.wait_ge(sem.om, 1)
        if t == 2:
            flatten(3)
            through(3)
        sc.activation(ks[:, 0:C], ws[:].indirect(om), Copy).then_inc(sem["kp%d" % u], 1)
        if t == 2:
            v.wait_ge(sem.x2, 16)
            v.quantize_mx(T.w2q[:, NEW:WIN], T.w2s[:, NEW:WIN], T.xb[:, 2048:3072]).then_inc(sem.qx2, 1)
            wrap(3)

    for name in LATE:
        k = int(name[1])
        v.wait_ge(sem[name], 16)
        if name[0] == "w":
            v.quantize_mx(T.wq[:, 128 * k:128 * k + 128], T.ws[:, 128 * k:128 * k + 128],
                          T.wb[:, 512 * k:512 * k + 512]).then_inc(sem["qw%d" % k], 1)
        else:
            v.quantize_mx(T.w3q[:, NEW:WIN], T.w3s[:, NEW:WIN], T.xb[:, 3072:4096]).then_inc(sem.qx3, 1)

    def product(t, src, ssrc, a, n, bank, done):
        te.matmul_mx(T.ps[:, 512 * bank:512 * bank + n], T.wq[:, 128 * t:128 * t + 128], T.ws[:, 128 * t:128 * t + 128],
                     src[:, a:a + n], ssrc[:, a:a + n], True, True).then_inc(done, 1)

    def ready(*names):
        for n in names:
            te.wait_ge(sem[n], 1)

    te.wait_ge(sem.qa, 2)
    ready("qw0")
    product(0, T.a0q, T.a0s, 0, C, 0, sem.m0)
    ready("qw3", "qx3")
    product(3, T.w3q, T.w3s, NEW, C, 4, sem.m3n)
    ready("qw1", "kc1", "kp1")
    product(1, T.w2q, T.w2s, 0, C, 1, sem.m1)
    ready("kc2", "kp2")
    product(3, T.w3q, T.w3s, 0, C, 3, sem.m3)
    ready("qw2")
    product(2, T.w3q, T.w3s, 0, C, 2, sem.m2)
    for b in (0, 1):
        sc.wait_ge(sem["m%d" % b], 1)
        sc.activation(T.yo[:, C * b:C * b + C], T.ps[:, 512 * b:512 * b + C], Copy).then_inc(sem["e%d" % b], 1)
    sc.wait_ge(sem.m3, 1)
    sc.activation(T.yw[:, 0:C], T.ps[:, 512 * 3:512 * 3 + C], Copy).then_inc(sem.e3, 1)
    v.wait_ge(sem.m3n, 1)
    v.tensor_copy(T.yw[:, NEW:WIN], T.ps[:, 512 * 4:512 * 4 + C]).then_inc(sem.e3, 1)
    v.wait_ge(sem.m2, 1)
    v.tensor_copy(T.yo[:, 2 * C:3 * C], T.ps[:, 512 * 2:512 * 2 + C]).then_inc(sem.e2, 1)
    sy.wait_ge(sem.leftc3, left)
    for b in (0, 1, 2):
        sy.wait_ge(sem["e%d" % b], 1)
        sy.dma_start(T.y[:, C * b:C * b + C], T.yo[:, C * b:C * b + C]).then_inc(sem.stored, 16)

    te.wait_ge(sem.lc3, got)
    te.wait_ge(sem.lp3, got)
    for i, (d, e) in enumerate(kept):
        a, n = C + CAP * d, max(128, CAP * (e - d))
        skip = CAP if CAP * (e - d) < 128 and d == 0 else 0
        product(3, T.w3q, T.w3s, a - skip, n, 5 + i, sem.m3m if i else sem.m3l)
        src, dst = T.ps[:, 512 * (5 + i) + skip:512 * (5 + i) + skip + CAP * (e - d)], T.yw[:, a:C + CAP * e]
        if i:
            sc.wait_ge(sem.m3m, 1)
            sc.activation(dst, src, Copy).then_inc(sem.e3l, 1)
        else:
            v.wait_ge(sem.m3l, 1)
            v.tensor_copy(dst, src).then_inc(sem.e3l, 1)
    for q in (v, sc):
        q.wait_ge(sem.e3, 2)
        q.wait_ge(sem.e3l, len(kept))
    v.tensor_copy(T.yo[:, 3 * C + 128:4 * C], T.yw[:].indirect(T.offm[:, 40:48])).then_inc(sem.fin, 1)
    sc.activation(T.yo[:, 3 * C:3 * C + 128], T.yw[:].indirect(T.offm[:, 32:40]), Copy).then_inc(sem.fin, 1)
    sy.wait_ge(sem.fin, 2)
    sy.dma_start(T.y[:, 3 * C:4 * C], T.yo[:, 3 * C:4 * C]).then_inc(sem.stored, 16)
    for t in (1, 2, 3):
        sy.wait_ge(sem["leftp%d" % t], left)
    sy.wait_ge(sem.stored, 64)
